import numpy as np
import ml_dtypes


def mxq(x, axis, fmt="e4m3"):
    dtype, down = {"e4m3": (ml_dtypes.float8_e4m3fn, 7), "e5m2": (ml_dtypes.float8_e5m2, 14)}[fmt]
    v = np.moveaxis(np.asarray(x, np.float32).astype(ml_dtypes.bfloat16).astype(np.float64), axis, -1)
    blocks = v.reshape(v.shape[:-1] + (-1, 32))
    amax = np.abs(blocks).max(-1, keepdims=True)
    byte = np.maximum(np.where(amax > 0, np.frexp(amax)[1] - 1 + 127, 0) - down, 1)
    scale = np.exp2(byte - 127.0)
    codes = (blocks / scale).astype(np.float32).astype(dtype).astype(np.float64)
    return np.moveaxis((codes * scale).reshape(v.shape), -1, axis)


WIDE = False


def mx_kscale(k):
    if not WIDE:
        return np.ones(k)
    levels = np.array([10, -10, 5, -5, 0])
    if k % 512:
        return np.exp2(np.random.permutation(np.resize(levels, k // 32))).repeat(32)
    a = np.empty((k // 512, 16))
    for p in range(k // 512):
        a[p, :8] = np.random.permutation(np.resize(levels, 8))
        for g in range(8):
            far = levels[np.abs(levels - a[p, g]) >= 10]
            a[p, g + 8] = far[np.random.randint(len(far))]
    return np.exp2(a.ravel()).repeat(32)


def f64(x):
    return np.asarray(x).astype(np.float64)


def striped8(idx):
    return np.asarray(idx).reshape(8, -1, 16).transpose(0, 2, 1).reshape(128, -1).astype(np.uint16)


def unstriped8(offs):
    return offs.reshape(8, 16, -1).transpose(0, 2, 1).reshape(8, -1).astype(np.int64)


def pick8(x, idx, run):
    r = np.arange(len(x))
    return x[r[:, None], idx[r % (8 * run) // run]]


E2M1 = np.array([0.0, 0.5, 1.0, 1.5, 2.0, 3.0, 4.0, 6.0, -0.0, -0.5, -1.0, -1.5, -2.0, -3.0, -4.0, -6.0])


def pack_weight(w, fmt):
    k, n = w.shape
    w = f64(np.asarray(w, np.float32).astype(ml_dtypes.bfloat16)).reshape(k // 32, 32, n)
    amax = np.abs(w).max(1)
    if fmt == "e4m3":
        byte = np.frexp(amax)[1] - 1 + 127 - 7
    else:
        mant, ex = np.frexp(amax / 6.0)
        byte = np.where(mant > 0.5, ex, ex - 1) + 127
    byte = np.clip(np.where(amax > 0, byte, 1), 1, 254)
    scaled = (w * np.exp2(127.0 - byte)[:, None, :]).reshape(k, n).astype(np.float32)
    by_word = np.ascontiguousarray(scaled.reshape(k // 512, 128, 4, n).transpose(0, 1, 3, 2))
    if fmt == "e4m3":
        words = by_word.astype(ml_dtypes.float8_e4m3fn).view(np.uint8)
    else:
        c = by_word.astype(ml_dtypes.float4_e2m1fn).view(np.uint8) & 0xF
        words = (c[..., 0::2] | (c[..., 1::2] << 4)).reshape(k // 512, 128, 2 * n)
    return np.ascontiguousarray(words), np.ascontiguousarray(byte.astype(np.uint8).reshape(k // 512, 16, n))


def unpack_weight(words, scales, fmt):
    g, _, n = scales.shape
    words = np.ascontiguousarray(words).reshape(g, 128, n, -1)
    if fmt == "e4m3":
        vals = words.view(ml_dtypes.float8_e4m3fn).astype(np.float64)
    else:
        nib = np.empty((g, 128, n, 4), np.uint8)
        nib[..., 0::2] = words & 0xF
        nib[..., 1::2] = words >> 4
        vals = E2M1[nib]
    vals = vals * np.repeat(np.exp2(scales.astype(np.float64) - 127.0), 8, axis=1)[..., None]
    return vals.transpose(0, 1, 3, 2).reshape(g * 512, n)


D, K, T, U, X, I, Q = 512, 512, 1024, 1024, 1024, 512, 128


def setup_inputs():
    n = np.random.standard_normal
    idx = np.stack([np.random.permutation(U)[:I] for _ in range(8)])
    idx2 = np.stack([np.random.permutation(U)[:I] for _ in range(8)])
    idx3 = np.stack([np.random.permutation(U)[:I] for _ in range(8)])
    idx4 = np.stack([np.random.permutation(T)[:I] for _ in range(8)])
    idx5 = np.stack([np.random.permutation(X)[:I] for _ in range(8)])
    idx6 = np.stack([np.random.permutation(X)[:I] for _ in range(8)])
    fd = mx_kscale(D)
    fk = mx_kscale(K)
    wqp = pack_weight(n((D, K)) * 1.0 / np.sqrt(D) * fd[:, None] * fk, "e4m3")
    cachep = pack_weight(n((K, T)) * 1.0 / np.sqrt(K) / fk[:, None], "e4m3")
    draftp = pack_weight(n((K, U)) * 1.0 / np.sqrt(K) / fk[:, None], "e2m1")
    archp = pack_weight(n((D, X)) * 1.0 / np.sqrt(D) * fd[:, None], "e4m3")
    return {
        "states": (n((D, Q)) * 0.95 / fd[:, None]).astype(np.float32),
        "wq_words": wqp[0],
        "wq_scales": wqp[1],
        "cache_words": cachep[0],
        "cache_scales": cachep[1],
        "draft_words": draftp[0],
        "draft_scales": draftp[1],
        "arch_words": archp[0],
        "arch_scales": archp[1],
        "offs": striped8(idx),
        "offs2": striped8(idx2),
        "offs3": striped8(idx3),
        "offs4": striped8(idx4),
        "offs5": striped8(idx5),
        "offs6": striped8(idx6),
    }


def reference(states, wq_words, wq_scales, cache_words, cache_scales, draft_words, draft_scales, arch_words, arch_scales, offs, offs2, offs3, offs4, offs5, offs6):
    idx = unstriped8(offs)
    idx2 = unstriped8(offs2)
    idx3 = unstriped8(offs3)
    idx4 = unstriped8(offs4)
    idx5 = unstriped8(offs5)
    idx6 = unstriped8(offs6)
    wqu = unpack_weight(wq_words, wq_scales, "e4m3")
    cacheu = unpack_weight(cache_words, cache_scales, "e4m3")
    draftu = unpack_weight(draft_words, draft_scales, "e2m1")
    archu = unpack_weight(arch_words, arch_scales, "e4m3")
    statesq = mxq(f64(states), 0, "e4m3")
    qv = wqu.T @ statesq
    qvq = mxq(qv, 0, "e4m3")
    a = qvq.T @ cacheu
    b = qvq.T @ draftu
    c0 = statesq.T @ archu
    nb = np.zeros((Q, U))
    nb[np.arange(Q)[:, None], idx2[np.arange(Q) % 128 // 16]] = pick8(b, idx, 16)
    w = pick8(nb, idx3, 16) + pick8(a, idx4, 16)
    f1 = np.zeros((Q, X))
    f1[np.arange(Q)[:, None], idx5[np.arange(Q) % 128 // 16]] = w
    cc = np.maximum(c0, f1)
    y = pick8(cc, idx6, 16) - w
    return y

from contextlib import ExitStack

import concourse.mybir as mybir

F32 = mybir.dt.float32
BF16 = mybir.dt.bfloat16
I32 = mybir.dt.int32
U32 = mybir.dt.uint32
U16 = mybir.dt.uint16
U8 = mybir.dt.uint8
FP8X4 = mybir.dt.float8_e4m3fn_x4
FP4X4 = mybir.dt.float4_e2m1fn_x4
COPY = mybir.ActivationFunctionType.Copy
ADD = mybir.AluOpType.add
SUB = mybir.AluOpType.subtract
MAX = mybir.AluOpType.max

P = 128
PACK = 4
K = 512
Q = 128
TOKENS = 1024
SLOTS = 512
BANK = 512
HALF = SLOTS // 2
LIST_COLS = SLOTS // 16

FLOPS = 2 * K * K * Q + 3 * 2 * K * Q * TOKENS


def tile_attend_beamstep_sidethree_kernel(
    tc, states, wq_words, wq_scales, cache_words, cache_scales, draft_words, draft_scales,
    arch_words, arch_scales, offs, offs2, offs3, offs4, offs5, offs6, out,
):
    nc = tc.nc
    with ExitStack() as ctx:
        lists = ctx.enter_context(tc.tile_pool(name="lists", bufs=1))
        sb = ctx.enter_context(tc.tile_pool(name="sb", bufs=1))
        ps = ctx.enter_context(tc.psum_pool(name="ps", bufs=1))

        def zeroed_plane(name, width):
            plane = sb.tile([P, width], U8, name=name, align_bytes=64)
            nc.vector.memset(plane[:].bitcast(U32), 0)
            return plane

        def load_plane(queue, plane, scales):
            for quad in range(4):
                queue.dma_start(
                    plane[32 * quad : 32 * quad + 4, :].bitcast(I32),
                    scales[0, 4 * quad : 4 * quad + 4, :].bitcast(I32),
                )

        def load_fp8_words(name, words, width):
            t = sb.tile([P, width], U32, name=name, align_bytes=64)
            nc.sync.dma_start(t[:].bitcast(I32), words[0].rearrange("p n t -> p (n t)").bitcast(I32))
            return t

        def load_list(name, src):
            t = lists.tile([P, LIST_COLS], U16, name=name)
            nc.sync.dma_start(t[:], src)
            return t

        def half_list(t, h):
            return t[:, h * LIST_COLS // 2 : (h + 1) * LIST_COLS // 2]

        wq_plane_raw = zeroed_plane("wq_plane_raw", K)
        draft_plane = zeroed_plane("draft_plane", TOKENS)
        cache_plane = zeroed_plane("cache_plane", TOKENS)
        arch_plane = zeroed_plane("arch_plane", TOKENS)
        nb = sb.tile([P, TOKENS], F32, name="nb")
        nc.vector.memset(nb[:], 0.0)
        f1 = sb.tile([P, TOKENS], F32, name="f1")
        nc.vector.memset(f1[:], 0.0)

        st_raw = sb.tile([P, PACK, Q], F32, name="st_raw")
        nc.sync.dma_start(st_raw[:], states.rearrange("(p j) q -> p j q", j=PACK))
        wq_raw = load_fp8_words("wq_raw", wq_words, K)
        load_plane(nc.sync, wq_plane_raw, wq_scales)
        draft_w = sb.tile([P, 2 * TOKENS], U8, name="draft_w", align_bytes=64)
        nc.sync.dma_start(draft_w[:].bitcast(I32), draft_words[0].bitcast(I32))
        load_plane(nc.sync, draft_plane, draft_scales)
        l1 = load_list("l1", offs)
        l2 = load_list("l2", offs2)
        cache_w = load_fp8_words("cache_w", cache_words, TOKENS)
        load_plane(nc.sync, cache_plane, cache_scales)
        l4 = load_list("l4", offs4)
        l3 = load_list("l3", offs3)
        arch_w = load_fp8_words("arch_w", arch_words, TOKENS)
        load_plane(nc.sync, arch_plane, arch_scales)
        l5 = load_list("l5", offs5)
        l6 = load_list("l6", offs6)

        wq_plane = sb.tile([P, K], U8, name="wq_plane", align_bytes=64)
        nc.vector.tensor_copy(
            wq_plane[:].rearrange("p (t m) -> p m t", t=PACK),
            wq_plane_raw[:].rearrange("p (m t) -> p m t", t=PACK),
        )

        st_bf = sb.tile([P, Q, PACK], BF16, name="st_bf", align_bytes=64)
        split = 80
        nc.vector.tensor_copy(st_bf[:, :split, :], st_raw[:, :, :split].rearrange("p j q -> p q j"))
        nc.scalar.activation(st_bf[:, split:, :], st_raw[:, :, split:].rearrange("p j q -> p q j"), COPY)
        st_codes = sb.tile([P, Q], U32, name="st_codes", align_bytes=64)
        st_plane = sb.tile([P, Q], U8, name="st_plane", align_bytes=64)
        nc.vector.quantize_mx(out=st_codes[:].bitcast(FP8X4), scales=st_plane[:], in_=st_bf[:].rearrange("p q j -> p (q j)"))

        wq_pairs = []
        for u in range(2):
            pair = sb.tile([P, 2, P], U32, name="wq_pair%d" % u, align_bytes=64)
            nc.scalar.copy(
                pair[:].rearrange("p e m -> p m e"),
                wq_raw[:].rearrange("p (m t) -> p m t", t=PACK)[:, :, 2 * u : 2 * u + 2],
            )
            wq_pairs.append(pair)

        qv_ps = ps.tile([P, PACK, Q], F32, name="qv_ps", tag="first")
        for t in range(PACK):
            nc.tensor.matmul_mx(
                out=qv_ps[:, t, :],
                lhsT=wq_pairs[t // 2][:, t % 2, :].bitcast(FP8X4),
                lhsT_scale=wq_plane[:, t * P : (t + 1) * P],
                rhs=st_codes[:].bitcast(FP8X4),
                rhs_scale=st_plane[:],
                start=True,
                stop=True,
            )
        qv_bf = sb.tile([P, Q, PACK], BF16, name="qv_bf", align_bytes=64)
        nc.scalar.copy(qv_bf[:], qv_ps[:].rearrange("p t q -> p q t"))
        qv_codes = sb.tile([P, Q], U32, name="qv_codes", align_bytes=64)
        qv_plane = sb.tile([P, Q], U8, name="qv_plane", align_bytes=64)
        nc.vector.quantize_mx(out=qv_codes[:].bitcast(FP8X4), scales=qv_plane[:], in_=qv_bf[:].rearrange("p q t -> p (q t)"))

        def scores(bank, codes, plane, moving, moving_plane):
            nc.tensor.matmul_mx(
                out=bank, lhsT=codes[:].bitcast(FP8X4), lhsT_scale=plane[:],
                rhs=moving, rhs_scale=moving_plane, start=True, stop=True,
            )

        b = sb.tile([P, TOKENS], F32, name="b")
        start = 0
        for c, step in enumerate((256, 256, 256, 128, 128)):
            cols = slice(start, start + step)
            bank = ps.tile([P, step], F32, name="b_ps%d" % c, tag="b_ps%d" % c)
            scores(bank[:], qv_codes, qv_plane, draft_w[:, 2 * start : 2 * (start + step)].bitcast(FP4X4), draft_plane[:, cols])
            start = start + step
            if c % 2 == 0:
                nc.vector.tensor_copy(b[:, cols], bank[:])
            else:
                nc.scalar.copy(b[:, cols], bank[:])

        picked = sb.tile([P, SLOTS], F32, name="picked")
        nc.vector.tensor_copy(picked[:, :HALF], b[:].indirect(half_list(l1, 0)))
        nc.scalar.activation(picked[:, HALF:], b[:].indirect(half_list(l1, 1)), COPY)
        nc.scalar.activation(nb[:].indirect(l2[:]), picked[:], COPY)

        a = sb.tile([P, TOKENS], F32, name="a")
        for c in range(TOKENS // BANK):
            cols = slice(c * BANK, (c + 1) * BANK)
            bank = ps.tile([P, BANK], F32, name="a_ps%d" % c, tag="first" if c == 0 else "b_ps0")
            scores(bank[:], qv_codes, qv_plane, cache_w[:, cols].bitcast(FP8X4), cache_plane[:, cols])
            nc.vector.tensor_copy(a[:, cols], bank[:])
        a_picked = sb.tile([P, SLOTS], F32, name="a_picked")
        nc.vector.tensor_copy(a_picked[:], a[:].indirect(l4[:]))

        c_banks = []
        for c in range(TOKENS // BANK):
            cols = slice(c * BANK, (c + 1) * BANK)
            bank = ps.tile([P, BANK], F32, name="c_ps%d" % c)
            scores(bank[:], st_codes, st_plane, arch_w[:, cols].bitcast(FP8X4), arch_plane[:, cols])
            c_banks.append(bank)

        w = []
        for h in range(2):
            wh = sb.tile([P, HALF], F32, name="w%d" % h)
            nc.vector.tensor_tensor(wh[:], nb[:].indirect(half_list(l3, h)), a_picked[:, h * HALF : (h + 1) * HALF], ADD)
            nc.scalar.activation(f1[:].indirect(half_list(l5, h)), wh[:], COPY)
            w.append(wh)

        cc = sb.tile([P, TOKENS], F32, name="cc")
        for c in range(TOKENS // BANK):
            cols = slice(c * BANK, (c + 1) * BANK)
            nc.vector.tensor_tensor(cc[:, cols], c_banks[c][:], f1[:, cols], MAX)

        y0 = sb.tile([P, HALF], F32, name="y0")
        nc.vector.tensor_tensor(y0[:], cc[:].indirect(half_list(l6, 0)), w[0][:], SUB)
        nc.sync.dma_start(out[:, :HALF], y0[:])
        cc_picked = sb.tile([P, HALF], F32, name="cc_picked")
        nc.scalar.activation(cc_picked[:], cc[:].indirect(half_list(l6, 1)), COPY)
        y1 = sb.tile([P, HALF], F32, name="y1")
        nc.vector.tensor_tensor(y1[:], cc_picked[:], w[1][:], SUB)
        nc.scalar.dma_start(out[:, HALF:], y1[:])
